import numpy as np
import ml_dtypes

BF16 = ml_dtypes.bfloat16


def bf(x):
    return np.asarray(x, np.float32).astype(BF16)


def f32(x):
    return np.asarray(x, np.float32)


def f64(x):
    return np.asarray(x).astype(np.float64)


def striped(idx):
    return np.tile(idx.reshape(-1, 16).T, (8, 1))


S, K, M, N = 256, 128, 256, 128


def setup_inputs():
    return {"base": bf(np.random.standard_normal((M, S))), "x": bf(np.random.standard_normal((K, N))), "w": bf(np.random.standard_normal((K, M)) / np.sqrt(K)), "b": f32(0.5 * np.random.standard_normal((M, 1))), "offs": striped(np.random.permutation(S)[:N])}


def reference(base, x, w, b, offs):
    idx = offs[:16].T.reshape(-1)
    z = f64(base).copy()
    z[:, idx] = f64(w).T @ f64(x)
    return np.tanh(z + f64(b))

@@ -1,0 +1,55 @@
+import concourse.mybir as mybir
+from concourse.masks import make_identity
+
+P = 128
+S = 256
+N = 128
+M = 256
+BLOCKS = M // P
+
+FLOPS = 2 * P * M * N
+
+BF16, F32, U16 = mybir.dt.bfloat16, mybir.dt.float32, mybir.dt.uint16
+TANH = mybir.ActivationFunctionType.Tanh
+
+
+def tile_scatter_matmul_kernel(tc, base, x, w, b, offs, out):
+    nc = tc.nc
+    with (
+        tc.tile_pool(name="held", bufs=1) as held,
+        tc.psum_pool(name="psum", bufs=1) as psum,
+    ):
+        offsets = held.tile([P, N // 16], U16, name="offsets")
+        nc.sync.dma_start(offsets[:], offs)
+
+        base_tiles = [held.tile([P, S], BF16, name=f"base{a}") for a in range(BLOCKS)]
+        nc.sync.dma_start(base_tiles[0][:], base[0:P, :])
+        nc.scalar.dma_start(base_tiles[1][:], base[P : 2 * P, :])
+        w_tile = held.tile([P, M], BF16, name="w_tile")
+        nc.sync.dma_start(w_tile[:], w)
+        x_tile = held.tile([P, N], BF16, name="x_tile")
+        nc.scalar.dma_start(x_tile[:], x)
+        bias = held.tile([P, BLOCKS], F32, name="bias")
+        with nc.allow_non_contiguous_dma(reason="one float32 bias value to a partition and block"):
+            nc.scalar.dma_start(bias[:], b.rearrange("(a p) o -> p (a o)", p=P))
+
+        identity = held.tile([P, P], BF16, name="identity")
+        make_identity(nc, identity[:])
+
+        windows = [psum.tile([P, S], F32, name=f"window{a}") for a in range(BLOCKS)]
+        for a in range(BLOCKS):
+            nc.tensor.matmul(windows[a][:], identity[:], base_tiles[a][:], start=True, stop=True)
+
+        for a in range(BLOCKS):
+            nc.tensor.matmul(
+                windows[a][:].indirect(offsets[:]),
+                w_tile[:, a * P : (a + 1) * P],
+                x_tile[:],
+                start=True,
+                stop=True,
+            )
+
+        for a in range(BLOCKS):
+            result = held.tile([P, S], F32, name=f"result{a}")
+            nc.scalar.activation(result[:], windows[a][:], TANH, bias=bias[:, a : a + 1])
+            nc.sync.dma_start(out[a * P : (a + 1) * P, :], result[:])

@@ -33,6 +33,10 @@ def tile_scatter_matmul_kernel(tc, base, x, w, b, offs, out):
         with nc.allow_non_contiguous_dma(reason="one float32 bias value to a partition and block"):
             nc.scalar.dma_start(bias[:], b.rearrange("(a p) o -> p (a o)", p=P))
 
+        warm = held.tile([P, 1], F32, name="warm")
+        nc.vector.memset(warm[:], 0.0)
+        nc.scalar.activation(warm[:], warm[:], TANH)
+
         identity = held.tile([P, P], BF16, name="identity")
         make_identity(nc, identity[:])
 

@@ -19,9 +19,6 @@ def tile_scatter_matmul_kernel(tc, base, x, w, b, offs, out):
         tc.tile_pool(name="held", bufs=1) as held,
         tc.psum_pool(name="psum", bufs=1) as psum,
     ):
-        offsets = held.tile([P, N // 16], U16, name="offsets")
-        nc.sync.dma_start(offsets[:], offs)
-
         base_tiles = [held.tile([P, S], BF16, name=f"base{a}") for a in range(BLOCKS)]
         nc.sync.dma_start(base_tiles[0][:], base[0:P, :])
         nc.scalar.dma_start(base_tiles[1][:], base[P : 2 * P, :])
@@ -29,6 +26,8 @@ def tile_scatter_matmul_kernel(tc, base, x, w, b, offs, out):
         nc.sync.dma_start(w_tile[:], w)
         x_tile = held.tile([P, N], BF16, name="x_tile")
         nc.scalar.dma_start(x_tile[:], x)
+        offsets = held.tile([P, N // 16], U16, name="offsets")
+        nc.sync.dma_start(offsets[:], offs)
         bias = held.tile([P, BLOCKS], F32, name="bias")
         with nc.allow_non_contiguous_dma(reason="one float32 bias value to a partition and block"):
             nc.scalar.dma_start(bias[:], b.rearrange("(a p) o -> p (a o)", p=P))

@@ -19,9 +19,11 @@ def tile_scatter_matmul_kernel(tc, base, x, w, b, offs, out):
         tc.tile_pool(name="held", bufs=1) as held,
         tc.psum_pool(name="psum", bufs=1) as psum,
     ):
+        base_blocks = base.rearrange("(p a) s -> p a s", a=BLOCKS)
+        out_blocks = out.rearrange("(p a) s -> p a s", a=BLOCKS)
         base_tiles = [held.tile([P, S], BF16, name=f"base{a}") for a in range(BLOCKS)]
-        nc.sync.dma_start(base_tiles[0][:], base[0:P, :])
-        nc.scalar.dma_start(base_tiles[1][:], base[P : 2 * P, :])
+        nc.sync.dma_start(base_tiles[0][:], base_blocks[:, 0, :])
+        nc.scalar.dma_start(base_tiles[1][:], base_blocks[:, 1, :])
         w_tile = held.tile([P, M], BF16, name="w_tile")
         nc.sync.dma_start(w_tile[:], w)
         x_tile = held.tile([P, N], BF16, name="x_tile")
@@ -29,8 +31,7 @@ def tile_scatter_matmul_kernel(tc, base, x, w, b, offs, out):
         offsets = held.tile([P, N // 16], U16, name="offsets")
         nc.sync.dma_start(offsets[:], offs)
         bias = held.tile([P, BLOCKS], F32, name="bias")
-        with nc.allow_non_contiguous_dma(reason="one float32 bias value to a partition and block"):
-            nc.scalar.dma_start(bias[:], b.rearrange("(a p) o -> p (a o)", p=P))
+        nc.scalar.dma_start(bias[:], b.rearrange("(p a) o -> p (a o)", a=BLOCKS))
 
         warm = held.tile([P, 1], F32, name="warm")
         nc.vector.memset(warm[:], 0.0)
@@ -43,10 +44,14 @@ def tile_scatter_matmul_kernel(tc, base, x, w, b, offs, out):
         for a in range(BLOCKS):
             nc.tensor.matmul(windows[a][:], identity[:], base_tiles[a][:], start=True, stop=True)
 
+        w_blocks = [held.tile([P, P], BF16, name=f"w_block{a}") for a in range(BLOCKS)]
+        for a in range(BLOCKS):
+            nc.vector.tensor_copy(w_blocks[a][:], w_tile[:, a::BLOCKS])
+
         for a in range(BLOCKS):
             nc.tensor.matmul(
                 windows[a][:].indirect(offsets[:]),
-                w_tile[:, a * P : (a + 1) * P],
+                w_blocks[a][:],
                 x_tile[:],
                 start=True,
                 stop=True,
@@ -55,4 +60,4 @@ def tile_scatter_matmul_kernel(tc, base, x, w, b, offs, out):
         for a in range(BLOCKS):
             result = held.tile([P, S], F32, name=f"result{a}")
             nc.scalar.activation(result[:], windows[a][:], TANH, bias=bias[:, a : a + 1])
-            nc.sync.dma_start(out[a * P : (a + 1) * P, :], result[:])
+            nc.sync.dma_start(out_blocks[:, a, :], result[:])

@@ -7,6 +7,9 @@ N = 128
 M = 256
 BLOCKS = M // P
 
+IDLE_REPEATS = 4
+IDLE_MATMULS = 2
+
 FLOPS = 2 * P * M * N
 
 BF16, F32, U16 = mybir.dt.bfloat16, mybir.dt.float32, mybir.dt.uint16
@@ -32,6 +35,18 @@ def tile_scatter_matmul_kernel(tc, base, x, w, b, offs, out):
         nc.sync.dma_start(offsets[:], offs)
         bias = held.tile([P, BLOCKS], F32, name="bias")
         nc.scalar.dma_start(bias[:], b.rearrange("(p a) o -> p (a o)", a=BLOCKS))
+
+        zeros = held.tile([P, P], BF16, name="zeros")
+        nc.vector.memset(zeros[:], 0.0)
+        idle_bank = psum.tile([P, IDLE_REPEATS, P], F32, name="idle_bank")
+        for i in range(IDLE_MATMULS):
+            nc.tensor.matmul(
+                idle_bank[:],
+                zeros[:],
+                zeros[:].unsqueeze(1).to_broadcast([P, IDLE_REPEATS, P]),
+                start=True,
+                stop=True,
+            )
 
         warm = held.tile([P, 1], F32, name="warm")
         nc.vector.memset(warm[:], 0.0)
@@ -60,4 +75,5 @@ def tile_scatter_matmul_kernel(tc, base, x, w, b, offs, out):
         for a in range(BLOCKS):
             result = held.tile([P, S], F32, name=f"result{a}")
             nc.scalar.activation(result[:], windows[a][:], TANH, bias=bias[:, a : a + 1])
-            nc.sync.dma_start(out_blocks[:, a, :], result[:])
+            store_queue = nc.scalar if a == BLOCKS - 1 else nc.sync
+            store_queue.dma_start(out_blocks[:, a, :], result[:])

@@ -7,6 +7,8 @@ N = 128
 M = 256
 BLOCKS = M // P
 
+ROW_ALIGN = 1024
+
 IDLE_REPEATS = 4
 IDLE_MATMULS = 2
 
@@ -24,19 +26,19 @@ def tile_scatter_matmul_kernel(tc, base, x, w, b, offs, out):
     ):
         base_blocks = base.rearrange("(p a) s -> p a s", a=BLOCKS)
         out_blocks = out.rearrange("(p a) s -> p a s", a=BLOCKS)
-        base_tiles = [held.tile([P, S], BF16, name=f"base{a}") for a in range(BLOCKS)]
+        base_tiles = [held.tile([P, S], BF16, name=f"base{a}", align_bytes=ROW_ALIGN) for a in range(BLOCKS)]
         nc.sync.dma_start(base_tiles[0][:], base_blocks[:, 0, :])
         nc.scalar.dma_start(base_tiles[1][:], base_blocks[:, 1, :])
-        w_tile = held.tile([P, M], BF16, name="w_tile")
+        w_tile = held.tile([P, M], BF16, name="w_tile", align_bytes=ROW_ALIGN)
         nc.sync.dma_start(w_tile[:], w)
-        x_tile = held.tile([P, N], BF16, name="x_tile")
+        x_tile = held.tile([P, N], BF16, name="x_tile", align_bytes=ROW_ALIGN)
         nc.scalar.dma_start(x_tile[:], x)
         offsets = held.tile([P, N // 16], U16, name="offsets")
         nc.sync.dma_start(offsets[:], offs)
         bias = held.tile([P, BLOCKS], F32, name="bias")
         nc.scalar.dma_start(bias[:], b.rearrange("(p a) o -> p (a o)", a=BLOCKS))
 
-        zeros = held.tile([P, P], BF16, name="zeros")
+        zeros = held.tile([P, P], BF16, name="zeros", align_bytes=ROW_ALIGN)
         nc.vector.memset(zeros[:], 0.0)
         idle_bank = psum.tile([P, IDLE_REPEATS, P], F32, name="idle_bank")
         for i in range(IDLE_MATMULS):
@@ -52,14 +54,14 @@ def tile_scatter_matmul_kernel(tc, base, x, w, b, offs, out):
         nc.vector.memset(warm[:], 0.0)
         nc.scalar.activation(warm[:], warm[:], TANH)
 
-        identity = held.tile([P, P], BF16, name="identity")
+        identity = held.tile([P, P], BF16, name="identity", align_bytes=ROW_ALIGN)
         make_identity(nc, identity[:])
 
         windows = [psum.tile([P, S], F32, name=f"window{a}") for a in range(BLOCKS)]
         for a in range(BLOCKS):
             nc.tensor.matmul(windows[a][:], identity[:], base_tiles[a][:], start=True, stop=True)
 
-        w_blocks = [held.tile([P, P], BF16, name=f"w_block{a}") for a in range(BLOCKS)]
+        w_blocks = [held.tile([P, P], BF16, name=f"w_block{a}", align_bytes=ROW_ALIGN) for a in range(BLOCKS)]
         for a in range(BLOCKS):
             nc.vector.tensor_copy(w_blocks[a][:], w_tile[:, a::BLOCKS])
 
@@ -73,7 +75,7 @@ def tile_scatter_matmul_kernel(tc, base, x, w, b, offs, out):
             )
 
         for a in range(BLOCKS):
-            result = held.tile([P, S], F32, name=f"result{a}")
+            result = held.tile([P, S], F32, name=f"result{a}", align_bytes=ROW_ALIGN)
             nc.scalar.activation(result[:], windows[a][:], TANH, bias=bias[:, a : a + 1])
             store_queue = nc.scalar if a == BLOCKS - 1 else nc.sync
             store_queue.dma_start(out_blocks[:, a, :], result[:])

@@ -6,6 +6,8 @@ S = 256
 N = 128
 M = 256
 BLOCKS = M // P
+PIECES = 2
+PIECE = N // PIECES
 
 ROW_ALIGN = 1024
 
@@ -66,13 +68,14 @@ def tile_scatter_matmul_kernel(tc, base, x, w, b, offs, out):
             nc.vector.tensor_copy(w_blocks[a][:], w_tile[:, a::BLOCKS])
 
         for a in range(BLOCKS):
-            nc.tensor.matmul(
-                windows[a][:].indirect(offsets[:]),
-                w_blocks[a][:],
-                x_tile[:],
-                start=True,
-                stop=True,
-            )
+            for piece in range(PIECES):
+                nc.tensor.matmul(
+                    windows[a][:].indirect(offsets[:, piece * PIECE // 16 : (piece + 1) * PIECE // 16]),
+                    w_blocks[a][:],
+                    x_tile[:, piece * PIECE : (piece + 1) * PIECE],
+                    start=True,
+                    stop=True,
+                )
 
         for a in range(BLOCKS):
             result = held.tile([P, S], F32, name=f"result{a}", align_bytes=ROW_ALIGN)

import concourse.mybir as mybir
from concourse.masks import make_identity

P = 128
S = 256
N = 128
M = 256
BLOCKS = M // P
PIECES = 2
PIECE = N // PIECES

ROW_ALIGN = 1024

IDLE_REPEATS = 4
IDLE_MATMULS = 2

FLOPS = 2 * P * M * N

BF16, F32, U16 = mybir.dt.bfloat16, mybir.dt.float32, mybir.dt.uint16
TANH = mybir.ActivationFunctionType.Tanh


def tile_scatter_matmul_kernel(tc, base, x, w, b, offs, out):
    nc = tc.nc
    with (
        tc.tile_pool(name="held", bufs=1) as held,
        tc.psum_pool(name="psum", bufs=1) as psum,
    ):
        base_blocks = base.rearrange("(p a) s -> p a s", a=BLOCKS)
        out_blocks = out.rearrange("(p a) s -> p a s", a=BLOCKS)
        base_tiles = [held.tile([P, S], BF16, name=f"base{a}", align_bytes=ROW_ALIGN) for a in range(BLOCKS)]
        nc.sync.dma_start(base_tiles[0][:], base_blocks[:, 0, :])
        nc.scalar.dma_start(base_tiles[1][:], base_blocks[:, 1, :])
        w_tile = held.tile([P, M], BF16, name="w_tile", align_bytes=ROW_ALIGN)
        nc.sync.dma_start(w_tile[:], w)
        x_tile = held.tile([P, N], BF16, name="x_tile", align_bytes=ROW_ALIGN)
        nc.scalar.dma_start(x_tile[:], x)
        offsets = held.tile([P, N // 16], U16, name="offsets")
        nc.sync.dma_start(offsets[:], offs)
        bias = held.tile([P, BLOCKS], F32, name="bias")
        nc.scalar.dma_start(bias[:], b.rearrange("(p a) o -> p (a o)", a=BLOCKS))

        zeros = held.tile([P, P], BF16, name="zeros", align_bytes=ROW_ALIGN)
        nc.vector.memset(zeros[:], 0.0)
        idle_bank = psum.tile([P, IDLE_REPEATS, P], F32, name="idle_bank")
        for i in range(IDLE_MATMULS):
            nc.tensor.matmul(
                idle_bank[:],
                zeros[:],
                zeros[:].unsqueeze(1).to_broadcast([P, IDLE_REPEATS, P]),
                start=True,
                stop=True,
            )

        warm = held.tile([P, 1], F32, name="warm")
        nc.vector.memset(warm[:], 0.0)
        nc.scalar.activation(warm[:], warm[:], TANH)

        identity = held.tile([P, P], BF16, name="identity", align_bytes=ROW_ALIGN)
        make_identity(nc, identity[:])

        windows = [psum.tile([P, S], F32, name=f"window{a}") for a in range(BLOCKS)]
        for a in range(BLOCKS):
            nc.tensor.matmul(windows[a][:], identity[:], base_tiles[a][:], start=True, stop=True)

        w_blocks = [held.tile([P, P], BF16, name=f"w_block{a}", align_bytes=ROW_ALIGN) for a in range(BLOCKS)]
        for a in range(BLOCKS):
            nc.vector.tensor_copy(w_blocks[a][:], w_tile[:, a::BLOCKS])

        for a in range(BLOCKS):
            for piece in range(PIECES):
                nc.tensor.matmul(
                    windows[a][:].indirect(offsets[:, piece * PIECE // 16 : (piece + 1) * PIECE // 16]),
                    w_blocks[a][:],
                    x_tile[:, piece * PIECE : (piece + 1) * PIECE],
                    start=True,
                    stop=True,
                )

        for a in range(BLOCKS):
            result = held.tile([P, S], F32, name=f"result{a}", align_bytes=ROW_ALIGN)
            nc.scalar.activation(result[:], windows[a][:], TANH, bias=bias[:, a : a + 1])
            store_queue = nc.scalar if a == BLOCKS - 1 else nc.sync
            store_queue.dma_start(out_blocks[:, a, :], result[:])
